import numpy as np
import ml_dtypes


def mxq(x, axis, fmt="e4m3"):
    dtype, down = {"e4m3": (ml_dtypes.float8_e4m3fn, 7), "e5m2": (ml_dtypes.float8_e5m2, 14)}[fmt]
    v = np.moveaxis(np.asarray(x, np.float32).astype(ml_dtypes.bfloat16).astype(np.float64), axis, -1)
    blocks = v.reshape(v.shape[:-1] + (-1, 32))
    amax = np.abs(blocks).max(-1, keepdims=True)
    byte = np.maximum(np.where(amax > 0, np.frexp(amax)[1] - 1 + 127, 0) - down, 1)
    scale = np.exp2(byte - 127.0)
    codes = (blocks / scale).astype(np.float32).astype(dtype).astype(np.float64)
    return np.moveaxis((codes * scale).reshape(v.shape), -1, axis)


WIDE = False


def mx_kscale(k):
    if not WIDE:
        return np.ones(k)
    levels = np.array([10, -10, 5, -5, 0])
    if k % 512:
        return np.exp2(np.random.permutation(np.resize(levels, k // 32))).repeat(32)
    a = np.empty((k // 512, 16))
    for p in range(k // 512):
        a[p, :8] = np.random.permutation(np.resize(levels, 8))
        for g in range(8):
            far = levels[np.abs(levels - a[p, g]) >= 10]
            a[p, g + 8] = far[np.random.randint(len(far))]
    return np.exp2(a.ravel()).repeat(32)


def f64(x):
    return np.asarray(x).astype(np.float64)


def striped(idx):
    return np.tile(idx.reshape(-1, 16).T, (8, 1)).astype(np.uint16)


def unstriped(offs):
    return offs[:16].T.reshape(-1).astype(np.int64)


def striped8(idx):
    return np.concatenate([x.reshape(-1, 16).T for x in idx]).astype(np.uint16)


def runs(offs, k):
    lists = np.stack([offs[16 * r : 16 * r + 16].T.reshape(-1) for r in range(8)]).astype(np.int64)
    return lists[np.arange(k) % 512 // 64]


def pack_weight(w):
    k, n = w.shape
    w = f64(np.asarray(w, np.float32).astype(ml_dtypes.bfloat16)).reshape(k // 32, 32, n)
    amax = np.abs(w).max(1)
    byte = np.clip(np.where(amax > 0, np.frexp(amax)[1] - 1 + 127 - 7, 1), 1, 254)
    scaled = (w * np.exp2(127.0 - byte)[:, None, :]).reshape(k, n).astype(np.float32)
    words = np.ascontiguousarray(scaled.reshape(k // 512, 128, 4, n).transpose(0, 1, 3, 2)).astype(ml_dtypes.float8_e4m3fn).view(np.uint8)
    return words, np.ascontiguousarray(byte.astype(np.uint8).reshape(k // 512, 16, n))


def unpack_weight(words, scales):
    g, p, n, _ = words.shape
    vals = np.ascontiguousarray(words).view(ml_dtypes.float8_e4m3fn).astype(np.float64) * np.repeat(np.exp2(scales.astype(np.float64) - 127.0), 8, axis=1)[..., None]
    return vals.transpose(0, 1, 3, 2).reshape(g * 512, n)


def sigmoid(v):
    return 1.0 / (1.0 + np.exp(-np.maximum(v, -700.0)))


K, T, S, N, G, H = 512, 2048, 512, 512, 2048, 512


def setup_inputs():
    n = np.random.standard_normal
    s = mx_kscale(K)[:, None]
    u = mx_kscale(S)
    packed_xT = pack_weight(n((K, T)) * s)
    packed_dT = pack_weight(n((K, G)) / s)
    return {
        "x_words": packed_xT[0],
        "x_scales": packed_xT[1],
        "d_words": packed_dT[0],
        "d_scales": packed_dT[1],
        "gn": (np.random.uniform(0.5, 1.5, (H, 1)) * u[:, None]).astype(np.float32),
        "w1": (n((H, N)) / np.sqrt(H) / u[:, None]).astype(np.float32),
        "offs": striped(np.random.permutation(T)[:S]),
        "k1": striped8(np.random.randint(0, G, (8, H))),
        "two": striped(np.random.permutation(T)[:S]),
        "n1": striped8(np.stack([np.random.permutation(S) for _ in range(8)])),
        "n2": striped8(np.stack([np.random.permutation(S) for _ in range(8)])),
        "n3": striped8(np.stack([np.random.permutation(S) for _ in range(8)])),
    }


def reference(x_words, x_scales, d_words, d_scales, gn, w1, offs, k1, two, n1, n2, n3):
    d_k1 = unpack_weight(d_words, d_scales)[np.arange(K)[:, None], runs(k1, K)]
    xq = unpack_weight(x_words, x_scales)[:, unstriped(offs)]
    a = 0.0625 * (d_k1.T @ xq)
    x_two = unpack_weight(x_words, x_scales)[:, unstriped(two)]
    b = 0.0625 * (d_k1.T @ x_two)
    z = f64(gn) * (a * (sigmoid(b[np.arange(H)[:, None], runs(n2, H)])) - (0.5 * (a[np.arange(H)[:, None], runs(n1, H)])))
    h = mxq(f64(w1), 0, "e4m3").T @ mxq(z, 0, "e4m3")
    st = h - (h[np.arange(N)[:, None], runs(n3, N)])
    return st - (0.5 * (st[np.arange(N)[:, None], runs(n3, N)]))

@@ -1,0 +1,223 @@
+from contextlib import ExitStack
+
+import concourse.mybir as mybir
+
+K, T, S, N, G, H = 512, 2048, 512, 512, 2048, 512
+FLOPS = 3 * 2 * 512 * 512 * 512
+
+F32 = mybir.dt.float32
+BF16 = mybir.dt.bfloat16
+I32 = mybir.dt.int32
+U32 = mybir.dt.uint32
+U16 = mybir.dt.uint16
+U8 = mybir.dt.uint8
+FP8X4 = mybir.dt.float8_e4m3fn_x4
+ALU = mybir.AluOpType
+ACT = mybir.ActivationFunctionType
+
+P = 128
+PACK = 4
+HALF = S // 2
+
+
+def tile_picked_twksgatebtwice_none_p_kernel(
+    tc, x_words, x_scales, d_words, d_scales, gn, w1, offs, k1, two, n1, n2, n3, out
+):
+    nc = tc.nc
+    with ExitStack() as ctx:
+        lists = ctx.enter_context(tc.tile_pool(name="lists", bufs=1))
+        sb = ctx.enter_context(tc.tile_pool(name="sb", bufs=1))
+        psum = ctx.enter_context(tc.psum_pool(name="psum", bufs=1))
+
+        def load_list(name, src):
+            tile = lists.tile([P, S // 16], U16, name=name)
+            nc.sync.dma_start(tile[:], src)
+            return tile
+
+        def load_words(name, src):
+            tile = sb.tile([P, T], U32, name=name)
+            nc.sync.dma_start(tile[:].bitcast(I32), src[0].rearrange("p c r -> p (c r)").bitcast(I32))
+            return tile
+
+        def half_of(list_tile, c):
+            return list_tile[:, c * HALF // 16 : (c + 1) * HALF // 16]
+
+        d_bytes = sb.tile([P, G], U8, name="d_bytes")
+        x_bytes = sb.tile([P, T], U8, name="x_bytes")
+        nc.vector.memset(d_bytes[:].bitcast(I32), 0)
+        nc.vector.memset(x_bytes[:].bitcast(I32), 0)
+
+        k1_sb = load_list("k1_sb", k1)
+        offs_sb = load_list("offs_sb", offs)
+        nc.sync.dma_start(d_bytes[0:P:8, :].bitcast(I32), d_scales[0].bitcast(I32))
+        for q in range(4):
+            nc.sync.dma_start(x_bytes[32 * q : 32 * q + 4, :].bitcast(I32), x_scales[0, 4 * q : 4 * q + 4, :].bitcast(I32))
+        d_table = load_words("d_table", d_words)
+        two_sb = load_list("two_sb", two)
+        n1_sb = load_list("n1_sb", n1)
+        n2_sb = load_list("n2_sb", n2)
+        x_table = load_words("x_table", x_words)
+        gn_sb = sb.tile([P, PACK], F32, name="gn_sb")
+        nc.sync.dma_start(gn_sb[:], gn.rearrange("(p t) o -> p (t o)", t=PACK))
+        w_raw = sb.tile([P, PACK, N], F32, name="w_raw")
+        nc.sync.dma_start(w_raw[:], w1.rearrange("(p j) n -> p j n", j=PACK))
+        n3_sb = load_list("n3_sb", n3)
+
+        key_bytes = sb.tile([P, H], U8, name="key_bytes")
+        nc.vector.tensor_copy(key_bytes[:], d_bytes[:].indirect(k1_sb[:]))
+        key_scales = sb.tile([P, H], U8, name="key_scales", align_bytes=64)
+        nc.vector.tensor_copy(
+            key_scales[:].rearrange("p (t m) -> p t m", t=PACK), key_bytes[:].rearrange("p (m t) -> p t m", t=PACK)
+        )
+        for i in range(1, 4):
+            nc.scalar.dma_start(key_scales[i:P:32, :].bitcast(I32), key_scales[8 * i : P : 32, :].bitcast(I32))
+
+        def pick_bytes(name, list_tile):
+            tile = sb.tile([P, S], U8, name=name, align_bytes=64)
+            nc.vector.tensor_copy(tile[:], x_bytes[:].indirect(list_tile[:]))
+            return tile
+
+        def pick_words(name, table, list_tile):
+            tile = sb.tile([P, S], U32, name=name, align_bytes=64)
+            nc.vector.tensor_copy(tile[:], table[:].indirect(list_tile[:]))
+            return tile
+
+        xa_scales = pick_bytes("xa_scales", offs_sb)
+        key_picked = pick_words("key_picked", d_table, k1_sb)
+        key_codes = sb.tile([P, H], U32, name="key_codes", align_bytes=64)
+        nc.vector.tensor_copy(
+            key_codes[:].rearrange("p (t g i) -> p g t i", t=PACK, i=4),
+            key_picked[:].rearrange("p (g i t) -> p g t i", t=PACK, i=4),
+        )
+        gain = sb.tile([P, PACK], F32, name="gain")
+        nc.vector.tensor_scalar(gain[:], gn_sb[:], 0.0625, None, ALU.mult)
+        xa_codes = pick_words("xa_codes", x_table, offs_sb)
+
+        def mx_product(tag, lhs_codes, lhs_scales, t, codes, scales, width):
+            bank = psum.tile([P, width], F32, name=tag, tag=tag)
+            cols = slice(t * P, (t + 1) * P)
+            nc.tensor.matmul_mx(
+                out=bank[:],
+                lhsT=lhs_codes[:, cols].bitcast(FP8X4),
+                lhsT_scale=lhs_scales[:, cols],
+                rhs=codes[:].bitcast(FP8X4),
+                rhs_scale=scales[:],
+                start=True,
+                stop=True,
+            )
+            return bank
+
+        a_sb = []
+        for t in range(PACK):
+            bank = mx_product("bank%d" % t, key_codes, key_scales, t, xa_codes, xa_scales, S)
+            a_t = sb.tile([P, S], F32, name="a%d" % t)
+            nc.scalar.activation(a_t[:], bank[:], ACT.Copy, scale=gain[:, t : t + 1])
+            a_sb.append(a_t)
+
+        xb_scales = pick_bytes("xb_scales", two_sb)
+        xb_codes = pick_words("xb_codes", x_table, two_sb)
+        gate = []
+        for t in range(PACK):
+            bank = mx_product("bank%d" % (4 + t), key_codes, key_scales, t, xb_codes, xb_scales, S)
+            g_t = sb.tile([P, S], F32, name="gate%d" % t)
+            nc.scalar.activation(g_t[:], bank[:], ACT.Sigmoid, scale=0.0625)
+            gate.append(g_t)
+
+        w_bf = sb.tile([P, N * PACK], BF16, name="w_bf", align_bytes=64)
+        for u in range(2):
+            ms = slice(u * 64, (u + 1) * 64)
+            nc.gpsimd.tensor_scalar(
+                w_bf[:].rearrange("p (t m j) -> p m t j", t=PACK, j=PACK)[:, ms],
+                w_raw[:].rearrange("p j (m t) -> p m t j", t=PACK)[:, ms],
+                1.0, 0.0, ALU.mult, ALU.add,
+            )
+
+        gated = [sb.tile([P, PACK, HALF], F32, name="gated%d" % c) for c in range(2)]
+        other = [sb.tile([P, PACK, HALF], F32, name="other%d" % c) for c in range(2)]
+
+        def gather_other(t, c):
+            window = a_sb[t][:].indirect(half_of(n1_sb, c))
+            if t == 0 and c == 0:
+                nc.vector.tensor_scalar(other[c][:, t, :], window, -0.5, 0.0, ALU.mult, ALU.add)
+            else:
+                nc.scalar.activation(other[c][:, t, :], window, ACT.Copy, scale=-0.5)
+
+        def gather_gated(t, c):
+            nc.vector.tensor_tensor(
+                gated[c][:, t, :], gate[t][:].indirect(half_of(n2_sb, c)), a_sb[t][:, c * HALF : (c + 1) * HALF], ALU.mult
+            )
+
+        z_bf = [sb.tile([P, HALF * PACK], BF16, name="z_bf%d" % c, align_bytes=64) for c in range(2)]
+        z_codes = [sb.tile([P, HALF], U32, name="z_codes%d" % c, align_bytes=64) for c in range(2)]
+        z_scales = [sb.tile([P, HALF], U8, name="z_scales%d" % c, align_bytes=64) for c in range(2)]
+
+        def combine(c):
+            nc.vector.tensor_tensor(
+                z_bf[c][:].rearrange("p (g i t) -> p g t i", t=PACK, i=2),
+                gated[c][:].rearrange("p t (g i) -> p g t i", i=2),
+                other[c][:].rearrange("p t (g i) -> p g t i", i=2),
+                ALU.add,
+            )
+
+        def quantize(c):
+            nc.vector.quantize_mx(out=z_codes[c][:].bitcast(FP8X4), scales=z_scales[c][:], in_=z_bf[c][:])
+
+        w_codes = sb.tile([P, N], U32, name="w_codes", align_bytes=64)
+        w_scales = sb.tile([P, N], U8, name="w_scales", align_bytes=64)
+        h_window = [sb.tile([P, S], F32, name="h_window%d" % t) for t in range(PACK)]
+        h_plain = [sb.tile([P, S], F32, name="h_plain%d" % t) for t in range(PACK)]
+
+        def second_product(c):
+            cols = slice(c * HALF, (c + 1) * HALF)
+            for t in range(PACK):
+                bank = mx_product("bank%d" % (4 * c + t), w_codes, w_scales, t, z_codes[c], z_scales[c], HALF)
+                nc.scalar.copy(h_window[t][:, cols], bank[:])
+                nc.scalar.copy(h_plain[t][:, cols], bank[:])
+
+        for c in range(2):
+            for t in range(PACK):
+                gather_other(t, c)
+        for t in range(PACK):
+            gather_gated(t, 0)
+        nc.vector.quantize_mx(out=w_codes[:].bitcast(FP8X4), scales=w_scales[:], in_=w_bf[:])
+        gather_gated(0, 1)
+        gather_gated(1, 1)
+        combine(0)
+        gather_gated(2, 1)
+        quantize(0)
+        second_product(0)
+        gather_gated(3, 1)
+        combine(1)
+        quantize(1)
+        second_product(1)
+
+        out_rows = out.rearrange("(p t) n -> p t n", t=PACK)
+        neg_st = [sb.tile([P, S], F32, name="neg_st%d" % t) for t in range(PACK)]
+        hop = [sb.tile([P, S], F32, name="hop%d" % t) for t in range(PACK)]
+        res = [sb.tile([P, S], F32, name="res%d" % t) for t in range(PACK)]
+
+        def first_hop(t):
+            for c in range(2):
+                cols = slice(c * HALF, (c + 1) * HALF)
+                nc.vector.tensor_tensor(
+                    neg_st[t][:, cols], h_window[t][:].indirect(half_of(n3_sb, c)), h_plain[t][:, cols], ALU.subtract
+                )
+            for c in range(2):
+                cols = slice(c * HALF, (c + 1) * HALF)
+                nc.scalar.activation(hop[t][:, cols], neg_st[t][:].indirect(half_of(n3_sb, c)), ACT.Copy, scale=0.5)
+
+        def finish(t, pieces):
+            width = S // pieces
+            for c in range(pieces):
+                cols = slice(c * width, (c + 1) * width)
+                nc.vector.tensor_tensor(res[t][:, cols], hop[t][:, cols], neg_st[t][:, cols], ALU.subtract)
+                nc.sync.dma_start(out_rows[:, t, cols], res[t][:, cols])
+
+        first_hop(0)
+        first_hop(1)
+        first_hop(2)
+        finish(0, 1)
+        first_hop(3)
+        finish(1, 1)
+        finish(2, 1)
+        finish(3, 2)

@@ -35,62 +35,81 @@ def tile_picked_twksgatebtwice_none_p_kernel(
             return tile
 
         def load_words(name, src):
-            tile = sb.tile([P, T], U32, name=name)
+            tile = sb.tile([P, T], U32, name=name, tag=name)
             nc.sync.dma_start(tile[:].bitcast(I32), src[0].rearrange("p c r -> p (c r)").bitcast(I32))
             return tile
 
         def half_of(list_tile, c):
             return list_tile[:, c * HALF // 16 : (c + 1) * HALF // 16]
 
+        def cols_of(c):
+            return slice(c * HALF, (c + 1) * HALF)
+
         d_bytes = sb.tile([P, G], U8, name="d_bytes")
         x_bytes = sb.tile([P, T], U8, name="x_bytes")
-        nc.vector.memset(d_bytes[:].bitcast(I32), 0)
-        nc.vector.memset(x_bytes[:].bitcast(I32), 0)
+
+        def load_bytes(tile, src):
+            rows = src[0].bitcast(I32)
+            nc.sync.dma_start(tile[:].bitcast(I32), rows.unsqueeze(1).to_broadcast([16, 8, T // 4]))
 
         k1_sb = load_list("k1_sb", k1)
-        offs_sb = load_list("offs_sb", offs)
-        nc.sync.dma_start(d_bytes[0:P:8, :].bitcast(I32), d_scales[0].bitcast(I32))
-        for q in range(4):
-            nc.sync.dma_start(x_bytes[32 * q : 32 * q + 4, :].bitcast(I32), x_scales[0, 4 * q : 4 * q + 4, :].bitcast(I32))
-        d_table = load_words("d_table", d_words)
+        load_bytes(d_bytes, d_scales)
         two_sb = load_list("two_sb", two)
-        n1_sb = load_list("n1_sb", n1)
-        n2_sb = load_list("n2_sb", n2)
+        load_bytes(x_bytes, x_scales)
+        offs_sb = load_list("offs_sb", offs)
+        d_table = load_words("d_table", d_words)
         x_table = load_words("x_table", x_words)
-        gn_sb = sb.tile([P, PACK], F32, name="gn_sb")
-        nc.sync.dma_start(gn_sb[:], gn.rearrange("(p t) o -> p (t o)", t=PACK))
-        w_raw = sb.tile([P, PACK, N], F32, name="w_raw")
-        nc.sync.dma_start(w_raw[:], w1.rearrange("(p j) n -> p j n", j=PACK))
+        n2_sb = load_list("n2_sb", n2)
+        n1_sb = load_list("n1_sb", n1)
         n3_sb = load_list("n3_sb", n3)
+        gn_sb = sb.tile([P, PACK], F32, name="gn_sb")
+        nc.gpsimd.dma_start(gn_sb[:], gn.rearrange("(p t) o -> p (t o)", t=PACK))
+        w_rows = w1.rearrange("(p j) n -> p j n", j=PACK)
+        w_bf = sb.tile([P, N * PACK], BF16, name="w_bf", align_bytes=64)
+
+        def load_weights(u, tag):
+            raw = sb.tile([P, PACK, N // 2], F32, name="w_raw%d" % u, tag=tag)
+            nc.sync.dma_start(raw[:], w_rows[:, :, u * N // 2 : (u + 1) * N // 2])
+            return raw
+
+        def round_weights(u, raw):
+            nc.gpsimd.tensor_scalar(
+                w_bf[:].rearrange("p (t m j) -> p m t j", t=PACK, j=PACK)[:, u * 64 : (u + 1) * 64],
+                raw[:].rearrange("p j (m t) -> p m t j", t=PACK),
+                1.0, 0.0, ALU.mult, ALU.add,
+            )
+
+        w_first = load_weights(0, "w_first")
 
         key_bytes = sb.tile([P, H], U8, name="key_bytes")
+        token_bytes = sb.tile([P, 2 * S], U8, name="token_bytes")
+        planes = sb.tile([P, H + 2 * S], U8, name="planes", align_bytes=64)
         nc.vector.tensor_copy(key_bytes[:], d_bytes[:].indirect(k1_sb[:]))
-        key_scales = sb.tile([P, H], U8, name="key_scales", align_bytes=64)
+        nc.vector.tensor_copy(token_bytes[:, 0:S], x_bytes[:].indirect(two_sb[:]))
         nc.vector.tensor_copy(
-            key_scales[:].rearrange("p (t m) -> p t m", t=PACK), key_bytes[:].rearrange("p (m t) -> p t m", t=PACK)
+            planes[:, 0:H].rearrange("p (t m) -> p t m", t=PACK), key_bytes[:].rearrange("p (m t) -> p t m", t=PACK)
         )
+        nc.vector.tensor_copy(token_bytes[:, S : 2 * S], x_bytes[:].indirect(offs_sb[:]))
+        nc.vector.tensor_copy(planes[:, H:].bitcast(I32), token_bytes[:].bitcast(I32))
         for i in range(1, 4):
-            nc.scalar.dma_start(key_scales[i:P:32, :].bitcast(I32), key_scales[8 * i : P : 32, :].bitcast(I32))
-
-        def pick_bytes(name, list_tile):
-            tile = sb.tile([P, S], U8, name=name, align_bytes=64)
-            nc.vector.tensor_copy(tile[:], x_bytes[:].indirect(list_tile[:]))
-            return tile
+            nc.scalar.dma_start(planes[i:P:32, :].bitcast(I32), planes[8 * i : P : 32, :].bitcast(I32))
+        key_scales = planes[:, 0:H]
+        xb_scales = planes[:, H : H + S]
+        xa_scales = planes[:, H + S : H + 2 * S]
 
         def pick_words(name, table, list_tile):
             tile = sb.tile([P, S], U32, name=name, align_bytes=64)
             nc.vector.tensor_copy(tile[:], table[:].indirect(list_tile[:]))
             return tile
 
-        xa_scales = pick_bytes("xa_scales", offs_sb)
         key_picked = pick_words("key_picked", d_table, k1_sb)
+        w_second = load_weights(1, "d_table")
         key_codes = sb.tile([P, H], U32, name="key_codes", align_bytes=64)
         nc.vector.tensor_copy(
             key_codes[:].rearrange("p (t g i) -> p g t i", t=PACK, i=4),
             key_picked[:].rearrange("p (g i t) -> p g t i", t=PACK, i=4),
         )
-        gain = sb.tile([P, PACK], F32, name="gain")
-        nc.vector.tensor_scalar(gain[:], gn_sb[:], 0.0625, None, ALU.mult)
+        xb_codes = pick_words("xb_codes", x_table, two_sb)
         xa_codes = pick_words("xa_codes", x_table, offs_sb)
 
         def mx_product(tag, lhs_codes, lhs_scales, t, codes, scales, width):
@@ -101,58 +120,72 @@ def tile_picked_twksgatebtwice_none_p_kernel(
                 lhsT=lhs_codes[:, cols].bitcast(FP8X4),
                 lhsT_scale=lhs_scales[:, cols],
                 rhs=codes[:].bitcast(FP8X4),
-                rhs_scale=scales[:],
+                rhs_scale=scales,
                 start=True,
                 stop=True,
             )
             return bank
 
-        a_sb = []
-        for t in range(PACK):
-            bank = mx_product("bank%d" % t, key_codes, key_scales, t, xa_codes, xa_scales, S)
-            a_t = sb.tile([P, S], F32, name="a%d" % t)
-            nc.scalar.activation(a_t[:], bank[:], ACT.Copy, scale=gain[:, t : t + 1])
-            a_sb.append(a_t)
+        gain = sb.tile([P, PACK], F32, name="gain")
+        nc.gpsimd.tensor_scalar(gain[:], gn_sb[:], 0.0625, 0.0, ALU.mult, ALU.add)
+        gate = [sb.tile([P, S], F32, name="gate%d" % t) for t in range(PACK)]
+        a_window = [sb.tile([P, S], F32, name="a%d" % t) for t in range(PACK)]
+        a_bank = {}
 
-        xb_scales = pick_bytes("xb_scales", two_sb)
-        xb_codes = pick_words("xb_codes", x_table, two_sb)
-        gate = []
-        for t in range(PACK):
-            bank = mx_product("bank%d" % (4 + t), key_codes, key_scales, t, xb_codes, xb_scales, S)
-            g_t = sb.tile([P, S], F32, name="gate%d" % t)
-            nc.scalar.activation(g_t[:], bank[:], ACT.Sigmoid, scale=0.0625)
-            gate.append(g_t)
+        def score_b(t):
+            bank = mx_product("bank%d" % t, key_codes, key_scales, t, xb_codes, xb_scales, S)
+            nc.scalar.activation(gate[t][:], bank[:], ACT.Sigmoid, scale=0.0625)
 
-        w_bf = sb.tile([P, N * PACK], BF16, name="w_bf", align_bytes=64)
-        for u in range(2):
-            ms = slice(u * 64, (u + 1) * 64)
-            nc.gpsimd.tensor_scalar(
-                w_bf[:].rearrange("p (t m j) -> p m t j", t=PACK, j=PACK)[:, ms],
-                w_raw[:].rearrange("p j (m t) -> p m t j", t=PACK)[:, ms],
-                1.0, 0.0, ALU.mult, ALU.add,
-            )
+        def score_a(t):
+            a_bank[t] = mx_product("bank%d" % (4 + t), key_codes, key_scales, t, xa_codes, xa_scales, S)
+            nc.scalar.activation(a_window[t][:], a_bank[t][:], ACT.Copy, scale=gain[:, t : t + 1])
 
+        score_b(0)
+        score_b(1)
+        score_a(0)
+        score_a(1)
+        for t in (2, 3):
+            score_b(t)
+            score_a(t)
+
+        round_weights(0, w_first)
+        round_weights(1, w_second)
+
+        def gather(on_vector, dst, window, list_tile, c):
+            picked = window[:].indirect(half_of(list_tile, c))
+            if on_vector:
+                nc.vector.tensor_copy(dst, picked)
+            else:
+                nc.scalar.activation(dst, picked, ACT.Copy)
+
+        gate_at = [sb.tile([P, HALF], F32, name="gate_at%d" % c) for c in range(2)]
         gated = [sb.tile([P, PACK, HALF], F32, name="gated%d" % c) for c in range(2)]
         other = [sb.tile([P, PACK, HALF], F32, name="other%d" % c) for c in range(2)]
 
-        def gather_other(t, c):
-            window = a_sb[t][:].indirect(half_of(n1_sb, c))
-            if t == 0 and c == 0:
-                nc.vector.tensor_scalar(other[c][:, t, :], window, -0.5, 0.0, ALU.mult, ALU.add)
+        def gated_product(t, c):
+            if (t, c) in ((0, 0), (0, 1)):
+                gather(True, gate_at[c][:], gate[t], n2_sb, c)
+                nc.vector.scalar_tensor_tensor(
+                    gated[c][:, t, :], a_bank[t][:, cols_of(c)], gain[:, t : t + 1], gate_at[c][:], ALU.mult, ALU.mult
+                )
             else:
-                nc.scalar.activation(other[c][:, t, :], window, ACT.Copy, scale=-0.5)
+                nc.vector.tensor_tensor(
+                    gated[c][:, t, :], gate[t][:].indirect(half_of(n2_sb, c)), a_window[t][:, cols_of(c)], ALU.mult
+                )
 
-        def gather_gated(t, c):
-            nc.vector.tensor_tensor(
-                gated[c][:, t, :], gate[t][:].indirect(half_of(n2_sb, c)), a_sb[t][:, c * HALF : (c + 1) * HALF], ALU.mult
-            )
+        def gather_other(t, c):
+            picked = a_window[t][:].indirect(half_of(n1_sb, c))
+            if (t, c) in ((3, 0),):
+                nc.vector.tensor_scalar(other[c][:, t, :], picked, -0.5, 0.0, ALU.mult, ALU.add)
+            else:
+                nc.scalar.activation(other[c][:, t, :], picked, ACT.Copy, scale=-0.5)
 
         z_bf = [sb.tile([P, HALF * PACK], BF16, name="z_bf%d" % c, align_bytes=64) for c in range(2)]
         z_codes = [sb.tile([P, HALF], U32, name="z_codes%d" % c, align_bytes=64) for c in range(2)]
         z_scales = [sb.tile([P, HALF], U8, name="z_scales%d" % c, align_bytes=64) for c in range(2)]
 
-        def combine(c):
-            nc.vector.tensor_tensor(
+        def combine(engine, c):
+            engine.tensor_tensor(
                 z_bf[c][:].rearrange("p (g i t) -> p g t i", t=PACK, i=2),
                 gated[c][:].rearrange("p t (g i) -> p g t i", i=2),
                 other[c][:].rearrange("p t (g i) -> p g t i", i=2),
@@ -165,59 +198,73 @@ def tile_picked_twksgatebtwice_none_p_kernel(
         w_codes = sb.tile([P, N], U32, name="w_codes", align_bytes=64)
         w_scales = sb.tile([P, N], U8, name="w_scales", align_bytes=64)
         h_window = [sb.tile([P, S], F32, name="h_window%d" % t) for t in range(PACK)]
-        h_plain = [sb.tile([P, S], F32, name="h_plain%d" % t) for t in range(PACK)]
+        h_bank = {}
 
         def second_product(c):
-            cols = slice(c * HALF, (c + 1) * HALF)
             for t in range(PACK):
-                bank = mx_product("bank%d" % (4 * c + t), w_codes, w_scales, t, z_codes[c], z_scales[c], HALF)
-                nc.scalar.copy(h_window[t][:, cols], bank[:])
-                nc.scalar.copy(h_plain[t][:, cols], bank[:])
+                h_bank[t, c] = mx_product("bank%d" % (4 * c + t), w_codes, w_scales, t, z_codes[c], z_scales[c][:], HALF)
+                nc.scalar.copy(h_window[t][:, cols_of(c)], h_bank[t, c][:])
 
+        gated_product(0, 0)
+        gated_product(0, 1)
+        for t in (1, 2):
+            gated_product(t, 0)
+            gated_product(t, 1)
+        gated_product(3, 0)
         for c in range(2):
             for t in range(PACK):
                 gather_other(t, c)
-        for t in range(PACK):
-            gather_gated(t, 0)
         nc.vector.quantize_mx(out=w_codes[:].bitcast(FP8X4), scales=w_scales[:], in_=w_bf[:])
-        gather_gated(0, 1)
-        gather_gated(1, 1)
-        combine(0)
-        gather_gated(2, 1)
+        combine(nc.vector, 0)
+        gated_product(3, 1)
         quantize(0)
         second_product(0)
-        gather_gated(3, 1)
-        combine(1)
+        combine(nc.vector, 1)
         quantize(1)
         second_product(1)
 
         out_rows = out.rearrange("(p t) n -> p t n", t=PACK)
-        neg_st = [sb.tile([P, S], F32, name="neg_st%d" % t) for t in range(PACK)]
-        hop = [sb.tile([P, S], F32, name="hop%d" % t) for t in range(PACK)]
+        hop1 = [sb.tile([P, S], F32, name="hop1_%d" % t) for t in range(PACK)]
+        st = [sb.tile([P, S], F32, name="st%d" % t) for t in range(PACK)]
+        hop2 = [sb.tile([P, S], F32, name="hop2_%d" % t) for t in range(PACK)]
         res = [sb.tile([P, S], F32, name="res%d" % t) for t in range(PACK)]
 
-        def first_hop(t):
-            for c in range(2):
-                cols = slice(c * HALF, (c + 1) * HALF)
-                nc.vector.tensor_tensor(
-                    neg_st[t][:, cols], h_window[t][:].indirect(half_of(n3_sb, c)), h_plain[t][:, cols], ALU.subtract
-                )
-            for c in range(2):
-                cols = slice(c * HALF, (c + 1) * HALF)
-                nc.scalar.activation(hop[t][:, cols], neg_st[t][:].indirect(half_of(n3_sb, c)), ACT.Copy, scale=0.5)
+        def first_hop(t, c):
+            gather((t, c) not in ((1, 0), (1, 1), (3, 0)), hop1[t][:, cols_of(c)], h_window[t], n3_sb, c)
 
-        def finish(t, pieces):
-            width = S // pieces
-            for c in range(pieces):
-                cols = slice(c * width, (c + 1) * width)
-                nc.vector.tensor_tensor(res[t][:, cols], hop[t][:, cols], neg_st[t][:, cols], ALU.subtract)
-                nc.sync.dma_start(out_rows[:, t, cols], res[t][:, cols])
+        def subtract(t):
+            for c in range(2):
+                nc.vector.tensor_tensor(st[t][:, cols_of(c)], h_bank[t, c][:], hop1[t][:, cols_of(c)], ALU.subtract)
 
-        first_hop(0)
-        first_hop(1)
-        first_hop(2)
-        finish(0, 1)
-        first_hop(3)
-        finish(1, 1)
-        finish(2, 1)
-        finish(3, 2)
+        def second_hop(t, c):
+            picked = st[t][:].indirect(half_of(n3_sb, c))
+            if (t, c) in ((3, 1),):
+                nc.vector.tensor_scalar(hop2[t][:, cols_of(c)], picked, -0.5, 0.0, ALU.mult, ALU.add)
+            else:
+                nc.scalar.activation(hop2[t][:, cols_of(c)], picked, ACT.Copy, scale=-0.5)
+
+        def finish(engine, t, cols):
+            engine.tensor_tensor(res[t][:, cols], st[t][:, cols], hop2[t][:, cols], ALU.add)
+            nc.sync.dma_start(out_rows[:, t, cols], res[t][:, cols])
+
+        for t in range(2):
+            first_hop(t, 0)
+            first_hop(t, 1)
+        for t in range(2):
+            subtract(t)
+            second_hop(t, 0)
+            second_hop(t, 1)
+            finish(nc.gpsimd, t, slice(0, S))
+        first_hop(2, 0)
+        first_hop(2, 1)
+        subtract(2)
+        first_hop(3, 0)
+        first_hop(3, 1)
+        subtract(3)
+        for t in (2, 3):
+            second_hop(t, 0)
+            second_hop(t, 1)
+        finish(nc.gpsimd, 2, cols_of(0))
+        finish(nc.vector, 2, cols_of(1))
+        finish(nc.vector, 3, cols_of(1))
+        finish(nc.vector, 3, cols_of(0))

@@ -18,6 +18,7 @@ ACT = mybir.ActivationFunctionType
 P = 128
 PACK = 4
 HALF = S // 2
+BANKS = 8
 
 
 def tile_picked_twksgatebtwice_none_p_kernel(
@@ -27,17 +28,31 @@ def tile_picked_twksgatebtwice_none_p_kernel(
     with ExitStack() as ctx:
         lists = ctx.enter_context(tc.tile_pool(name="lists", bufs=1))
         sb = ctx.enter_context(tc.tile_pool(name="sb", bufs=1))
-        psum = ctx.enter_context(tc.psum_pool(name="psum", bufs=1))
+        ring = ctx.enter_context(tc.tile_pool(name="ring", bufs=2))
+        psum = ctx.enter_context(tc.psum_pool(name="psum", bufs=BANKS))
 
         def load_list(name, src):
             tile = lists.tile([P, S // 16], U16, name=name)
             nc.sync.dma_start(tile[:], src)
             return tile
 
+        def load_bytes(name, src):
+            tile = sb.tile([P, T], U8, name=name)
+            rows = src[0].bitcast(I32)
+            nc.sync.dma_start(tile[:].bitcast(I32), rows.unsqueeze(1).to_broadcast([16, 8, T // 4]))
+            return tile
+
         def load_words(name, src):
-            tile = sb.tile([P, T], U32, name=name, tag=name)
+            tile = sb.tile([P, T], U32, name=name)
             nc.sync.dma_start(tile[:].bitcast(I32), src[0].rearrange("p c r -> p (c r)").bitcast(I32))
             return tile
+
+        w_rows = w1.rearrange("(p j) n -> p j n", j=PACK)
+
+        def load_weights(u, tag):
+            raw = sb.tile([P, PACK, N // 2], F32, name="w_raw%d" % u, tag=tag)
+            nc.sync.dma_start(raw[:], w_rows[:, :, u * N // 2 : (u + 1) * N // 2])
+            return raw
 
         def half_of(list_tile, c):
             return list_tile[:, c * HALF // 16 : (c + 1) * HALF // 16]
@@ -45,18 +60,11 @@ def tile_picked_twksgatebtwice_none_p_kernel(
         def cols_of(c):
             return slice(c * HALF, (c + 1) * HALF)
 
-        d_bytes = sb.tile([P, G], U8, name="d_bytes")
-        x_bytes = sb.tile([P, T], U8, name="x_bytes")
-
-        def load_bytes(tile, src):
-            rows = src[0].bitcast(I32)
-            nc.sync.dma_start(tile[:].bitcast(I32), rows.unsqueeze(1).to_broadcast([16, 8, T // 4]))
-
-        k1_sb = load_list("k1_sb", k1)
-        load_bytes(d_bytes, d_scales)
+        x_bytes = load_bytes("x_bytes", x_scales)
         two_sb = load_list("two_sb", two)
-        load_bytes(x_bytes, x_scales)
         offs_sb = load_list("offs_sb", offs)
+        d_bytes = load_bytes("d_bytes", d_scales)
+        k1_sb = load_list("k1_sb", k1)
         d_table = load_words("d_table", d_words)
         x_table = load_words("x_table", x_words)
         n2_sb = load_list("n2_sb", n2)
@@ -64,62 +72,48 @@ def tile_picked_twksgatebtwice_none_p_kernel(
         n3_sb = load_list("n3_sb", n3)
         gn_sb = sb.tile([P, PACK], F32, name="gn_sb")
         nc.gpsimd.dma_start(gn_sb[:], gn.rearrange("(p t) o -> p (t o)", t=PACK))
-        w_rows = w1.rearrange("(p j) n -> p j n", j=PACK)
-        w_bf = sb.tile([P, N * PACK], BF16, name="w_bf", align_bytes=64)
+        w_raw = [load_weights(0, "w_first")]
 
-        def load_weights(u, tag):
-            raw = sb.tile([P, PACK, N // 2], F32, name="w_raw%d" % u, tag=tag)
-            nc.sync.dma_start(raw[:], w_rows[:, :, u * N // 2 : (u + 1) * N // 2])
-            return raw
-
-        def round_weights(u, raw):
-            nc.gpsimd.tensor_scalar(
-                w_bf[:].rearrange("p (t m j) -> p m t j", t=PACK, j=PACK)[:, u * 64 : (u + 1) * 64],
-                raw[:].rearrange("p j (m t) -> p m t j", t=PACK),
-                1.0, 0.0, ALU.mult, ALU.add,
-            )
-
-        w_first = load_weights(0, "w_first")
-
-        key_bytes = sb.tile([P, H], U8, name="key_bytes")
+        key_bytes = sb.tile([P, H], U8, name="key_bytes", tag="key_bytes")
         token_bytes = sb.tile([P, 2 * S], U8, name="token_bytes")
         planes = sb.tile([P, H + 2 * S], U8, name="planes", align_bytes=64)
-        nc.vector.tensor_copy(key_bytes[:], d_bytes[:].indirect(k1_sb[:]))
         nc.vector.tensor_copy(token_bytes[:, 0:S], x_bytes[:].indirect(two_sb[:]))
+        nc.vector.tensor_copy(token_bytes[:, S : 2 * S], x_bytes[:].indirect(offs_sb[:]))
+        nc.vector.tensor_copy(key_bytes[:], d_bytes[:].indirect(k1_sb[:]))
+        nc.vector.tensor_copy(planes[:, H:].bitcast(I32), token_bytes[:].bitcast(I32))
         nc.vector.tensor_copy(
             planes[:, 0:H].rearrange("p (t m) -> p t m", t=PACK), key_bytes[:].rearrange("p (m t) -> p t m", t=PACK)
         )
-        nc.vector.tensor_copy(token_bytes[:, S : 2 * S], x_bytes[:].indirect(offs_sb[:]))
-        nc.vector.tensor_copy(planes[:, H:].bitcast(I32), token_bytes[:].bitcast(I32))
         for i in range(1, 4):
-            nc.scalar.dma_start(planes[i:P:32, :].bitcast(I32), planes[8 * i : P : 32, :].bitcast(I32))
+            nc.sync.dma_start(planes[i:P:32, :].bitcast(I32), planes[8 * i : P : 32, :].bitcast(I32))
+        w_raw.append(load_weights(1, "key_bytes"))
+
+        key_picked = sb.tile([P, H], U32, name="key_picked")
+        key_codes = sb.tile([P, H], U32, name="key_codes", align_bytes=64)
+        for c in range(2):
+            nc.vector.tensor_copy(key_picked[:, cols_of(c)], d_table[:].indirect(half_of(k1_sb, c)))
+        for c in range(2):
+            nc.vector.tensor_copy(
+                key_codes[:].rearrange("p (t g i) -> p g t i", t=PACK, i=4)[:, 16 * c : 16 * (c + 1)],
+                key_picked[:, cols_of(c)].rearrange("p (g i t) -> p g t i", t=PACK, i=4),
+            )
+        xb_codes = sb.tile([P, S], U32, name="xb_codes", align_bytes=64)
+        xa_codes = sb.tile([P, S], U32, name="xa_codes", align_bytes=64)
+        for codes, list_tile in ((xb_codes, two_sb), (xa_codes, offs_sb)):
+            for c in range(2):
+                nc.vector.tensor_copy(codes[:, cols_of(c)], x_table[:].indirect(half_of(list_tile, c)))
         key_scales = planes[:, 0:H]
         xb_scales = planes[:, H : H + S]
         xa_scales = planes[:, H + S : H + 2 * S]
 
-        def pick_words(name, table, list_tile):
-            tile = sb.tile([P, S], U32, name=name, align_bytes=64)
-            nc.vector.tensor_copy(tile[:], table[:].indirect(list_tile[:]))
-            return tile
-
-        key_picked = pick_words("key_picked", d_table, k1_sb)
-        w_second = load_weights(1, "d_table")
-        key_codes = sb.tile([P, H], U32, name="key_codes", align_bytes=64)
-        nc.vector.tensor_copy(
-            key_codes[:].rearrange("p (t g i) -> p g t i", t=PACK, i=4),
-            key_picked[:].rearrange("p (g i t) -> p g t i", t=PACK, i=4),
-        )
-        xb_codes = pick_words("xb_codes", x_table, two_sb)
-        xa_codes = pick_words("xa_codes", x_table, offs_sb)
-
-        def mx_product(tag, lhs_codes, lhs_scales, t, codes, scales, width):
-            bank = psum.tile([P, width], F32, name=tag, tag=tag)
-            cols = slice(t * P, (t + 1) * P)
+        def mx_product(lhs_codes, lhs_scales, t, codes, scales):
+            bank = psum.tile([P, HALF], F32, name="bank")
+            rows = slice(t * P, (t + 1) * P)
             nc.tensor.matmul_mx(
                 out=bank[:],
-                lhsT=lhs_codes[:, cols].bitcast(FP8X4),
-                lhsT_scale=lhs_scales[:, cols],
-                rhs=codes[:].bitcast(FP8X4),
+                lhsT=lhs_codes[:, rows].bitcast(FP8X4),
+                lhsT_scale=lhs_scales[:, rows],
+                rhs=codes.bitcast(FP8X4),
                 rhs_scale=scales,
                 start=True,
                 stop=True,
@@ -128,143 +122,170 @@ def tile_picked_twksgatebtwice_none_p_kernel(
 
         gain = sb.tile([P, PACK], F32, name="gain")
         nc.gpsimd.tensor_scalar(gain[:], gn_sb[:], 0.0625, 0.0, ALU.mult, ALU.add)
+        w_bf = sb.tile([P, N * PACK], BF16, name="w_bf", align_bytes=64)
+        w_dealt = w_bf[:].rearrange("p (t m j) -> p m t j", t=PACK, j=PACK)
+        w_halves = [raw[:].rearrange("p j (m t) -> p m t j", t=PACK) for raw in w_raw]
+        nc.gpsimd.tensor_scalar(w_dealt[:, 0:64], w_halves[0], 1.0, 0.0, ALU.mult, ALU.add)
+        nc.vector.tensor_copy(w_dealt[:, 64:128], w_halves[1])
+
         gate = [sb.tile([P, S], F32, name="gate%d" % t) for t in range(PACK)]
-        a_window = [sb.tile([P, S], F32, name="a%d" % t) for t in range(PACK)]
-        a_bank = {}
+        a_rows = [sb.tile([P, S], F32, name="a_rows%d" % t) for t in range(PACK)]
 
-        def score_b(t):
-            bank = mx_product("bank%d" % t, key_codes, key_scales, t, xb_codes, xb_scales, S)
-            nc.scalar.activation(gate[t][:], bank[:], ACT.Sigmoid, scale=0.0625)
+        def score_b(t, c):
+            bank = mx_product(key_codes, key_scales, t, xb_codes[:, cols_of(c)], xb_scales[:, cols_of(c)])
+            nc.scalar.activation(gate[t][:, cols_of(c)], bank[:], ACT.Sigmoid, scale=0.0625)
 
-        def score_a(t):
-            a_bank[t] = mx_product("bank%d" % (4 + t), key_codes, key_scales, t, xa_codes, xa_scales, S)
-            nc.scalar.activation(a_window[t][:], a_bank[t][:], ACT.Copy, scale=gain[:, t : t + 1])
+        def score_a(t, c):
+            bank = mx_product(key_codes, key_scales, t, xa_codes[:, cols_of(c)], xa_scales[:, cols_of(c)])
+            nc.scalar.activation(a_rows[t][:, cols_of(c)], bank[:], ACT.Copy, scale=gain[:, t : t + 1])
 
-        score_b(0)
-        score_b(1)
-        score_a(0)
-        score_a(1)
+        score_b(0, 0)
+        score_b(1, 0)
+        score_b(0, 1)
+        score_b(1, 1)
+        score_a(0, 0)
+        score_a(1, 0)
         for t in (2, 3):
-            score_b(t)
-            score_a(t)
+            score_b(t, 0)
+            score_b(t, 1)
+            score_a(t, 0)
+        for t in range(PACK):
+            score_a(t, 1)
 
-        round_weights(0, w_first)
-        round_weights(1, w_second)
-
-        def gather(on_vector, dst, window, list_tile, c):
-            picked = window[:].indirect(half_of(list_tile, c))
-            if on_vector:
-                nc.vector.tensor_copy(dst, picked)
-            else:
-                nc.scalar.activation(dst, picked, ACT.Copy)
-
-        gate_at = [sb.tile([P, HALF], F32, name="gate_at%d" % c) for c in range(2)]
-        gated = [sb.tile([P, PACK, HALF], F32, name="gated%d" % c) for c in range(2)]
+        gated_ring = sb.tile([P, 2 * PACK - 1, HALF], F32, name="gated_ring", tag="key_bytes")
+        gated = [gated_ring[:, 0:PACK, :], gated_ring[:, PACK - 1 : 2 * PACK - 1, :]]
         other = [sb.tile([P, PACK, HALF], F32, name="other%d" % c) for c in range(2)]
 
-        def gated_product(t, c):
-            if (t, c) in ((0, 0), (0, 1)):
-                gather(True, gate_at[c][:], gate[t], n2_sb, c)
-                nc.vector.scalar_tensor_tensor(
-                    gated[c][:, t, :], a_bank[t][:, cols_of(c)], gain[:, t : t + 1], gate_at[c][:], ALU.mult, ALU.mult
-                )
+        def gated_product(t, c, j, width):
+            first = c * HALF + j
+            picked = gate[t][:].indirect(n2_sb[:, first // 16 : (first + width) // 16])
+            nc.vector.tensor_tensor(gated[c][:, t, j : j + width], picked, a_rows[t][:, first : first + width], ALU.mult)
+
+        def gather_scaled(on_vector, dst, window, list_tile, c):
+            picked = window[:].indirect(half_of(list_tile, c))
+            if on_vector:
+                nc.vector.tensor_scalar(dst, picked, -0.5, 0.0, ALU.mult, ALU.add)
             else:
-                nc.vector.tensor_tensor(
-                    gated[c][:, t, :], gate[t][:].indirect(half_of(n2_sb, c)), a_window[t][:, cols_of(c)], ALU.mult
-                )
+                nc.scalar.activation(dst, picked, ACT.Copy, scale=-0.5)
 
         def gather_other(t, c):
-            picked = a_window[t][:].indirect(half_of(n1_sb, c))
-            if (t, c) in ((3, 0),):
-                nc.vector.tensor_scalar(other[c][:, t, :], picked, -0.5, 0.0, ALU.mult, ALU.add)
-            else:
-                nc.scalar.activation(other[c][:, t, :], picked, ACT.Copy, scale=-0.5)
+            gather_scaled((t, c) in ((3, 0),), other[c][:, t, :], a_rows[t], n1_sb, c)
 
         z_bf = [sb.tile([P, HALF * PACK], BF16, name="z_bf%d" % c, align_bytes=64) for c in range(2)]
         z_codes = [sb.tile([P, HALF], U32, name="z_codes%d" % c, align_bytes=64) for c in range(2)]
         z_scales = [sb.tile([P, HALF], U8, name="z_scales%d" % c, align_bytes=64) for c in range(2)]
 
-        def combine(engine, c):
-            engine.tensor_tensor(
-                z_bf[c][:].rearrange("p (g i t) -> p g t i", t=PACK, i=2),
-                gated[c][:].rearrange("p t (g i) -> p g t i", i=2),
-                other[c][:].rearrange("p t (g i) -> p g t i", i=2),
+        def combine(c, j, width):
+            nc.vector.tensor_tensor(
+                z_bf[c][:, PACK * j : PACK * (j + width)].rearrange("p (g i t) -> p g t i", t=PACK, i=2),
+                gated[c][:, :, j : j + width].rearrange("p t (g i) -> p g t i", i=2),
+                other[c][:, :, j : j + width].rearrange("p t (g i) -> p g t i", i=2),
                 ALU.add,
             )
 
-        def quantize(c):
-            nc.vector.quantize_mx(out=z_codes[c][:].bitcast(FP8X4), scales=z_scales[c][:], in_=z_bf[c][:])
+        def quantize(c, j, width):
+            nc.vector.quantize_mx(
+                out=z_codes[c][:, j : j + width].bitcast(FP8X4),
+                scales=z_scales[c][:, j : j + width],
+                in_=z_bf[c][:, PACK * j : PACK * (j + width)],
+            )
 
         w_codes = sb.tile([P, N], U32, name="w_codes", align_bytes=64)
         w_scales = sb.tile([P, N], U8, name="w_scales", align_bytes=64)
-        h_window = [sb.tile([P, S], F32, name="h_window%d" % t) for t in range(PACK)]
+        neg_h = [sb.tile([P, S], F32, name="neg_h%d" % t) for t in range(PACK)]
+        h_left = [sb.tile([P, HALF], F32, name="h_left%d" % t) for t in range(PACK)]
         h_bank = {}
 
-        def second_product(c):
-            for t in range(PACK):
-                h_bank[t, c] = mx_product("bank%d" % (4 * c + t), w_codes, w_scales, t, z_codes[c], z_scales[c][:], HALF)
-                nc.scalar.copy(h_window[t][:, cols_of(c)], h_bank[t, c][:])
+        def product_left(t):
+            bank = mx_product(w_codes, w_scales, t, z_codes[0][:], z_scales[0][:])
+            nc.scalar.activation(neg_h[t][:, cols_of(0)], bank[:], ACT.Copy, scale=-1.0)
+            nc.scalar.copy(h_left[t][:], bank[:])
 
-        gated_product(0, 0)
-        gated_product(0, 1)
-        for t in (1, 2):
-            gated_product(t, 0)
-            gated_product(t, 1)
-        gated_product(3, 0)
+        def product_right(t):
+            h_bank[t, 1] = mx_product(w_codes, w_scales, t, z_codes[1][:], z_scales[1][:])
+
+        def negate_right(engine, t):
+            if engine == "V":
+                nc.vector.tensor_scalar(neg_h[t][:, cols_of(1)], h_bank[t, 1][:], -1.0, None, ALU.mult)
+            else:
+                nc.scalar.activation(neg_h[t][:, cols_of(1)], h_bank[t, 1][:], ACT.Copy, scale=-1.0)
+
+        for t in range(PACK):
+            gated_product(t, 0, 0, HALF)
+        gated_product(1, 1, 0, HALF)
+        gated_product(2, 1, 0, HALF)
         for c in range(2):
             for t in range(PACK):
                 gather_other(t, c)
+        gated_product(3, 1, 0, HALF)
         nc.vector.quantize_mx(out=w_codes[:].bitcast(FP8X4), scales=w_scales[:], in_=w_bf[:])
-        combine(nc.vector, 0)
-        gated_product(3, 1)
-        quantize(0)
-        second_product(0)
-        combine(nc.vector, 1)
-        quantize(1)
-        second_product(1)
+        combine(0, 0, HALF)
+        quantize(0, 0, HALF)
+        for t in range(PACK):
+            product_left(t)
+        for j in (0, HALF // 2):
+            gated_product(0, 1, j, HALF // 2)
+        for j in (0, HALF // 2):
+            combine(1, j, HALF // 2)
+        for j in (0, HALF // 2):
+            quantize(1, j, HALF // 2)
 
         out_rows = out.rearrange("(p t) n -> p t n", t=PACK)
-        hop1 = [sb.tile([P, S], F32, name="hop1_%d" % t) for t in range(PACK)]
-        st = [sb.tile([P, S], F32, name="st%d" % t) for t in range(PACK)]
-        hop2 = [sb.tile([P, S], F32, name="hop2_%d" % t) for t in range(PACK)]
-        res = [sb.tile([P, S], F32, name="res%d" % t) for t in range(PACK)]
+        hop1 = {}
+        st = [sb.tile([P, S], F32, name="st%d" % t, tag="st%d" % t) for t in range(PACK)]
+        hop2 = [sb.tile([P, S], F32, name="hop2_%d" % t, tag="hop2_%d" % t) for t in range(PACK)]
 
-        def first_hop(t, c):
-            gather((t, c) not in ((1, 0), (1, 1), (3, 0)), hop1[t][:, cols_of(c)], h_window[t], n3_sb, c)
+        def fused_hop(t):
+            nc.vector.tensor_tensor(st[t][:, cols_of(0)], neg_h[t][:].indirect(half_of(n3_sb, 0)), h_left[t][:], ALU.add)
 
-        def subtract(t):
-            for c in range(2):
-                nc.vector.tensor_tensor(st[t][:, cols_of(c)], h_bank[t, c][:], hop1[t][:, cols_of(c)], ALU.subtract)
-
-        def second_hop(t, c):
-            picked = st[t][:].indirect(half_of(n3_sb, c))
-            if (t, c) in ((3, 1),):
-                nc.vector.tensor_scalar(hop2[t][:, cols_of(c)], picked, -0.5, 0.0, ALU.mult, ALU.add)
+        def first_hop(engine, t, c):
+            hop1[t, c] = ring.tile([P, HALF], F32, name="hop1")
+            picked = neg_h[t][:].indirect(half_of(n3_sb, c))
+            if engine == "S":
+                nc.scalar.activation(hop1[t, c][:], picked, ACT.Copy)
             else:
-                nc.scalar.activation(hop2[t][:, cols_of(c)], picked, ACT.Copy, scale=-0.5)
+                nc.vector.tensor_copy(hop1[t, c][:], picked)
 
-        def finish(engine, t, cols):
-            engine.tensor_tensor(res[t][:, cols], st[t][:, cols], hop2[t][:, cols], ALU.add)
-            nc.sync.dma_start(out_rows[:, t, cols], res[t][:, cols])
+        def add_hop(t, c):
+            nc.vector.tensor_tensor(st[t][:, cols_of(c)], h_bank[t, c][:], hop1[t, c][:], ALU.add)
 
+        def second_hop(engine, t, c):
+            gather_scaled(engine == "V", hop2[t][:, cols_of(c)], st[t], n3_sb, c)
+
+        def finish(engine, t, cols, res):
+            engine.tensor_tensor(res[:, cols], st[t][:, cols], hop2[t][:, cols], ALU.add)
+            nc.sync.dma_start(out_rows[:, t, cols], res[:, cols])
+
+        for t in range(PACK):
+            product_right(t)
+        negate_right("V", 0)
+        negate_right("S", 1)
+        fused_hop(0)
+        first_hop("S", 0, 1)
+        negate_right("S", 2)
+        fused_hop(1)
+        add_hop(0, 1)
+        first_hop("S", 1, 1)
+        negate_right("S", 3)
+        fused_hop(2)
+        add_hop(1, 1)
         for t in range(2):
-            first_hop(t, 0)
-            first_hop(t, 1)
-        for t in range(2):
-            subtract(t)
-            second_hop(t, 0)
-            second_hop(t, 1)
-            finish(nc.gpsimd, t, slice(0, S))
-        first_hop(2, 0)
-        first_hop(2, 1)
-        subtract(2)
-        first_hop(3, 0)
-        first_hop(3, 1)
-        subtract(3)
-        for t in (2, 3):
-            second_hop(t, 0)
-            second_hop(t, 1)
-        finish(nc.gpsimd, 2, cols_of(0))
-        finish(nc.vector, 2, cols_of(1))
-        finish(nc.vector, 3, cols_of(1))
-        finish(nc.vector, 3, cols_of(0))
+            second_hop("S", t, 0)
+            second_hop("S", t, 1)
+            res = sb.tile([P, S], F32, name="res%d" % t)
+            finish(nc.gpsimd, t, slice(0, S), res)
+        fused_hop(3)
+        first_hop("V", 2, 1)
+        first_hop("V", 3, 1)
+        add_hop(2, 1)
+        add_hop(3, 1)
+        second_hop("S", 2, 0)
+        second_hop("S", 2, 1)
+        second_hop("V", 3, 1)
+        second_hop("S", 3, 0)
+        res2 = sb.tile([P, S], F32, name="res2", tag="st1")
+        res3 = sb.tile([P, S], F32, name="res3", tag="hop2_1")
+        finish(nc.vector, 2, cols_of(0), res2)
+        finish(nc.vector, 2, cols_of(1), res2)
+        finish(nc.vector, 3, cols_of(1), res3)
+        finish(nc.vector, 3, cols_of(0), res3)

@@ -107,7 +107,7 @@ def tile_picked_twksgatebtwice_none_p_kernel(
         xa_scales = planes[:, H + S : H + 2 * S]
 
         def mx_product(lhs_codes, lhs_scales, t, codes, scales):
-            bank = psum.tile([P, HALF], F32, name="bank")
+            bank = psum.tile([P, codes.shape[1]], F32, name="bank")
             rows = slice(t * P, (t + 1) * P)
             nc.tensor.matmul_mx(
                 out=bank[:],
@@ -201,14 +201,15 @@ def tile_picked_twksgatebtwice_none_p_kernel(
             nc.scalar.activation(neg_h[t][:, cols_of(0)], bank[:], ACT.Copy, scale=-1.0)
             nc.scalar.copy(h_left[t][:], bank[:])
 
-        def product_right(t):
-            h_bank[t, 1] = mx_product(w_codes, w_scales, t, z_codes[1][:], z_scales[1][:])
+        def product_right(t, j, width):
+            h_bank[t, j] = mx_product(w_codes, w_scales, t, z_codes[1][:, j : j + width], z_scales[1][:, j : j + width])
 
-        def negate_right(engine, t):
+        def negate_right(engine, t, j, width):
+            dst = neg_h[t][:, HALF + j : HALF + j + width]
             if engine == "V":
-                nc.vector.tensor_scalar(neg_h[t][:, cols_of(1)], h_bank[t, 1][:], -1.0, None, ALU.mult)
+                nc.vector.tensor_scalar(dst, h_bank[t, j][:], -1.0, None, ALU.mult)
             else:
-                nc.scalar.activation(neg_h[t][:, cols_of(1)], h_bank[t, 1][:], ACT.Copy, scale=-1.0)
+                nc.scalar.activation(dst, h_bank[t, j][:], ACT.Copy, scale=-1.0)
 
         for t in range(PACK):
             gated_product(t, 0, 0, HALF)
@@ -219,8 +220,10 @@ def tile_picked_twksgatebtwice_none_p_kernel(
                 gather_other(t, c)
         gated_product(3, 1, 0, HALF)
         nc.vector.quantize_mx(out=w_codes[:].bitcast(FP8X4), scales=w_scales[:], in_=w_bf[:])
-        combine(0, 0, HALF)
-        quantize(0, 0, HALF)
+        for j in (0, HALF // 2):
+            combine(0, j, HALF // 2)
+        for j in (0, HALF // 2):
+            quantize(0, j, HALF // 2)
         for t in range(PACK):
             product_left(t)
         for j in (0, HALF // 2):
@@ -233,7 +236,10 @@ def tile_picked_twksgatebtwice_none_p_kernel(
         out_rows = out.rearrange("(p t) n -> p t n", t=PACK)
         hop1 = {}
         st = [sb.tile([P, S], F32, name="st%d" % t, tag="st%d" % t) for t in range(PACK)]
-        hop2 = [sb.tile([P, S], F32, name="hop2_%d" % t, tag="hop2_%d" % t) for t in range(PACK)]
+        hop2 = [sb.tile([P, S], F32, name="hop2_%d" % t) for t in (0, 2, 3)]
+        hop2_1 = [sb.tile([P, HALF], F32, name="hop2_1_%d" % c, tag="hop2_1_%d" % c) for c in range(2)]
+        hop2_at = {(t, c): tile[:, cols_of(c)] for t, tile in zip((0, 2, 3), hop2) for c in range(2)}
+        hop2_at[1, 0], hop2_at[1, 1] = hop2_1[0][:], hop2_1[1][:]
 
         def fused_hop(t):
             nc.vector.tensor_tensor(st[t][:, cols_of(0)], neg_h[t][:].indirect(half_of(n3_sb, 0)), h_left[t][:], ALU.add)
@@ -246,46 +252,49 @@ def tile_picked_twksgatebtwice_none_p_kernel(
             else:
                 nc.vector.tensor_copy(hop1[t, c][:], picked)
 
-        def add_hop(t, c):
-            nc.vector.tensor_tensor(st[t][:, cols_of(c)], h_bank[t, c][:], hop1[t, c][:], ALU.add)
+        def add_hop(t, j, width):
+            nc.vector.tensor_tensor(
+                st[t][:, HALF + j : HALF + j + width], h_bank[t, j][:], hop1[t, 1][:, j : j + width], ALU.add
+            )
 
         def second_hop(engine, t, c):
-            gather_scaled(engine == "V", hop2[t][:, cols_of(c)], st[t], n3_sb, c)
+            gather_scaled(engine == "V", hop2_at[t, c], st[t], n3_sb, c)
 
-        def finish(engine, t, cols, res):
-            engine.tensor_tensor(res[:, cols], st[t][:, cols], hop2[t][:, cols], ALU.add)
-            nc.sync.dma_start(out_rows[:, t, cols], res[:, cols])
+        def finish(engine, t, cols, hop, res):
+            engine.tensor_tensor(res, st[t][:, cols], hop, ALU.add)
+            nc.sync.dma_start(out_rows[:, t, cols], res)
 
-        for t in range(PACK):
-            product_right(t)
-        negate_right("V", 0)
-        negate_right("S", 1)
+        for j in (0, HALF // 2):
+            product_right(0, j, HALF // 2)
+            negate_right("V", 0, j, HALF // 2)
+        for t in range(1, PACK):
+            product_right(t, 0, HALF)
+        negate_right("S", 1, 0, HALF)
         fused_hop(0)
         first_hop("S", 0, 1)
-        negate_right("S", 2)
+        negate_right("S", 2, 0, HALF)
         fused_hop(1)
-        add_hop(0, 1)
+        add_hop(0, 0, HALF // 2)
+        add_hop(0, HALF // 2, HALF // 2)
         first_hop("S", 1, 1)
-        negate_right("S", 3)
+        negate_right("S", 3, 0, HALF)
         fused_hop(2)
-        add_hop(1, 1)
+        add_hop(1, 0, HALF)
+        fused_hop(3)
         for t in range(2):
             second_hop("S", t, 0)
             second_hop("S", t, 1)
-            res = sb.tile([P, S], F32, name="res%d" % t)
-            finish(nc.gpsimd, t, slice(0, S), res)
-        fused_hop(3)
+        early = sb.tile([P, 3 * HALF], F32, name="early")
+        finish(nc.gpsimd, 0, slice(0, S), hop2[0][:], early[:, 0:S])
+        finish(nc.gpsimd, 1, cols_of(0), hop2_at[1, 0], early[:, S:])
         first_hop("V", 2, 1)
         first_hop("V", 3, 1)
-        add_hop(2, 1)
-        add_hop(3, 1)
+        add_hop(2, 0, HALF)
+        add_hop(3, 0, HALF)
         second_hop("S", 2, 0)
         second_hop("S", 2, 1)
         second_hop("V", 3, 1)
         second_hop("S", 3, 0)
-        res2 = sb.tile([P, S], F32, name="res2", tag="st1")
-        res3 = sb.tile([P, S], F32, name="res3", tag="hop2_1")
-        finish(nc.vector, 2, cols_of(0), res2)
-        finish(nc.vector, 2, cols_of(1), res2)
-        finish(nc.vector, 3, cols_of(1), res3)
-        finish(nc.vector, 3, cols_of(0), res3)
+        late = sb.tile([P, 5, HALF], F32, name="late", tag="hop2_1_0")
+        for k, (t, c) in enumerate(((1, 1), (2, 0), (2, 1), (3, 1), (3, 0))):
+            finish(nc.vector, t, cols_of(c), hop2_at[t, c], late[:, k, :])

@@ -60,14 +60,16 @@ def tile_picked_twksgatebtwice_none_p_kernel(
         def cols_of(c):
             return slice(c * HALF, (c + 1) * HALF)
 
+        d_bytes = sb.tile([P, G], U8, name="d_bytes")
+        nc.vector.memset(d_bytes[:].bitcast(I32), 0)
         x_bytes = load_bytes("x_bytes", x_scales)
         two_sb = load_list("two_sb", two)
         offs_sb = load_list("offs_sb", offs)
-        d_bytes = load_bytes("d_bytes", d_scales)
         k1_sb = load_list("k1_sb", k1)
+        n2_sb = load_list("n2_sb", n2)
+        nc.sync.dma_start(d_bytes[0:P:8, :].bitcast(I32), d_scales[0].bitcast(I32))
         d_table = load_words("d_table", d_words)
         x_table = load_words("x_table", x_words)
-        n2_sb = load_list("n2_sb", n2)
         n1_sb = load_list("n1_sb", n1)
         n3_sb = load_list("n3_sb", n3)
         gn_sb = sb.tile([P, PACK], F32, name="gn_sb")

from contextlib import ExitStack

import concourse.mybir as mybir

K, T, S, N, G, H = 512, 2048, 512, 512, 2048, 512
FLOPS = 3 * 2 * 512 * 512 * 512

F32 = mybir.dt.float32
BF16 = mybir.dt.bfloat16
I32 = mybir.dt.int32
U32 = mybir.dt.uint32
U16 = mybir.dt.uint16
U8 = mybir.dt.uint8
FP8X4 = mybir.dt.float8_e4m3fn_x4
ALU = mybir.AluOpType
ACT = mybir.ActivationFunctionType

P = 128
PACK = 4
HALF = S // 2
BANKS = 8


def tile_picked_twksgatebtwice_none_p_kernel(
    tc, x_words, x_scales, d_words, d_scales, gn, w1, offs, k1, two, n1, n2, n3, out
):
    nc = tc.nc
    with ExitStack() as ctx:
        lists = ctx.enter_context(tc.tile_pool(name="lists", bufs=1))
        sb = ctx.enter_context(tc.tile_pool(name="sb", bufs=1))
        ring = ctx.enter_context(tc.tile_pool(name="ring", bufs=2))
        psum = ctx.enter_context(tc.psum_pool(name="psum", bufs=BANKS))

        def load_list(name, src):
            tile = lists.tile([P, S // 16], U16, name=name)
            nc.sync.dma_start(tile[:], src)
            return tile

        def load_bytes(name, src):
            tile = sb.tile([P, T], U8, name=name)
            rows = src[0].bitcast(I32)
            nc.sync.dma_start(tile[:].bitcast(I32), rows.unsqueeze(1).to_broadcast([16, 8, T // 4]))
            return tile

        def load_words(name, src):
            tile = sb.tile([P, T], U32, name=name)
            nc.sync.dma_start(tile[:].bitcast(I32), src[0].rearrange("p c r -> p (c r)").bitcast(I32))
            return tile

        w_rows = w1.rearrange("(p j) n -> p j n", j=PACK)

        def load_weights(u, tag):
            raw = sb.tile([P, PACK, N // 2], F32, name="w_raw%d" % u, tag=tag)
            nc.sync.dma_start(raw[:], w_rows[:, :, u * N // 2 : (u + 1) * N // 2])
            return raw

        def half_of(list_tile, c):
            return list_tile[:, c * HALF // 16 : (c + 1) * HALF // 16]

        def cols_of(c):
            return slice(c * HALF, (c + 1) * HALF)

        d_bytes = sb.tile([P, G], U8, name="d_bytes")
        nc.vector.memset(d_bytes[:].bitcast(I32), 0)
        x_bytes = load_bytes("x_bytes", x_scales)
        two_sb = load_list("two_sb", two)
        offs_sb = load_list("offs_sb", offs)
        k1_sb = load_list("k1_sb", k1)
        n2_sb = load_list("n2_sb", n2)
        nc.sync.dma_start(d_bytes[0:P:8, :].bitcast(I32), d_scales[0].bitcast(I32))
        d_table = load_words("d_table", d_words)
        x_table = load_words("x_table", x_words)
        n1_sb = load_list("n1_sb", n1)
        n3_sb = load_list("n3_sb", n3)
        gn_sb = sb.tile([P, PACK], F32, name="gn_sb")
        nc.gpsimd.dma_start(gn_sb[:], gn.rearrange("(p t) o -> p (t o)", t=PACK))
        w_raw = [load_weights(0, "w_first")]

        key_bytes = sb.tile([P, H], U8, name="key_bytes", tag="key_bytes")
        token_bytes = sb.tile([P, 2 * S], U8, name="token_bytes")
        planes = sb.tile([P, H + 2 * S], U8, name="planes", align_bytes=64)
        nc.vector.tensor_copy(token_bytes[:, 0:S], x_bytes[:].indirect(two_sb[:]))
        nc.vector.tensor_copy(token_bytes[:, S : 2 * S], x_bytes[:].indirect(offs_sb[:]))
        nc.vector.tensor_copy(key_bytes[:], d_bytes[:].indirect(k1_sb[:]))
        nc.vector.tensor_copy(planes[:, H:].bitcast(I32), token_bytes[:].bitcast(I32))
        nc.vector.tensor_copy(
            planes[:, 0:H].rearrange("p (t m) -> p t m", t=PACK), key_bytes[:].rearrange("p (m t) -> p t m", t=PACK)
        )
        for i in range(1, 4):
            nc.sync.dma_start(planes[i:P:32, :].bitcast(I32), planes[8 * i : P : 32, :].bitcast(I32))
        w_raw.append(load_weights(1, "key_bytes"))

        key_picked = sb.tile([P, H], U32, name="key_picked")
        key_codes = sb.tile([P, H], U32, name="key_codes", align_bytes=64)
        for c in range(2):
            nc.vector.tensor_copy(key_picked[:, cols_of(c)], d_table[:].indirect(half_of(k1_sb, c)))
        for c in range(2):
            nc.vector.tensor_copy(
                key_codes[:].rearrange("p (t g i) -> p g t i", t=PACK, i=4)[:, 16 * c : 16 * (c + 1)],
                key_picked[:, cols_of(c)].rearrange("p (g i t) -> p g t i", t=PACK, i=4),
            )
        xb_codes = sb.tile([P, S], U32, name="xb_codes", align_bytes=64)
        xa_codes = sb.tile([P, S], U32, name="xa_codes", align_bytes=64)
        for codes, list_tile in ((xb_codes, two_sb), (xa_codes, offs_sb)):
            for c in range(2):
                nc.vector.tensor_copy(codes[:, cols_of(c)], x_table[:].indirect(half_of(list_tile, c)))
        key_scales = planes[:, 0:H]
        xb_scales = planes[:, H : H + S]
        xa_scales = planes[:, H + S : H + 2 * S]

        def mx_product(lhs_codes, lhs_scales, t, codes, scales):
            bank = psum.tile([P, codes.shape[1]], F32, name="bank")
            rows = slice(t * P, (t + 1) * P)
            nc.tensor.matmul_mx(
                out=bank[:],
                lhsT=lhs_codes[:, rows].bitcast(FP8X4),
                lhsT_scale=lhs_scales[:, rows],
                rhs=codes.bitcast(FP8X4),
                rhs_scale=scales,
                start=True,
                stop=True,
            )
            return bank

        gain = sb.tile([P, PACK], F32, name="gain")
        nc.gpsimd.tensor_scalar(gain[:], gn_sb[:], 0.0625, 0.0, ALU.mult, ALU.add)
        w_bf = sb.tile([P, N * PACK], BF16, name="w_bf", align_bytes=64)
        w_dealt = w_bf[:].rearrange("p (t m j) -> p m t j", t=PACK, j=PACK)
        w_halves = [raw[:].rearrange("p j (m t) -> p m t j", t=PACK) for raw in w_raw]
        nc.gpsimd.tensor_scalar(w_dealt[:, 0:64], w_halves[0], 1.0, 0.0, ALU.mult, ALU.add)
        nc.vector.tensor_copy(w_dealt[:, 64:128], w_halves[1])

        gate = [sb.tile([P, S], F32, name="gate%d" % t) for t in range(PACK)]
        a_rows = [sb.tile([P, S], F32, name="a_rows%d" % t) for t in range(PACK)]

        def score_b(t, c):
            bank = mx_product(key_codes, key_scales, t, xb_codes[:, cols_of(c)], xb_scales[:, cols_of(c)])
            nc.scalar.activation(gate[t][:, cols_of(c)], bank[:], ACT.Sigmoid, scale=0.0625)

        def score_a(t, c):
            bank = mx_product(key_codes, key_scales, t, xa_codes[:, cols_of(c)], xa_scales[:, cols_of(c)])
            nc.scalar.activation(a_rows[t][:, cols_of(c)], bank[:], ACT.Copy, scale=gain[:, t : t + 1])

        score_b(0, 0)
        score_b(1, 0)
        score_b(0, 1)
        score_b(1, 1)
        score_a(0, 0)
        score_a(1, 0)
        for t in (2, 3):
            score_b(t, 0)
            score_b(t, 1)
            score_a(t, 0)
        for t in range(PACK):
            score_a(t, 1)

        gated_ring = sb.tile([P, 2 * PACK - 1, HALF], F32, name="gated_ring", tag="key_bytes")
        gated = [gated_ring[:, 0:PACK, :], gated_ring[:, PACK - 1 : 2 * PACK - 1, :]]
        other = [sb.tile([P, PACK, HALF], F32, name="other%d" % c) for c in range(2)]

        def gated_product(t, c, j, width):
            first = c * HALF + j
            picked = gate[t][:].indirect(n2_sb[:, first // 16 : (first + width) // 16])
            nc.vector.tensor_tensor(gated[c][:, t, j : j + width], picked, a_rows[t][:, first : first + width], ALU.mult)

        def gather_scaled(on_vector, dst, window, list_tile, c):
            picked = window[:].indirect(half_of(list_tile, c))
            if on_vector:
                nc.vector.tensor_scalar(dst, picked, -0.5, 0.0, ALU.mult, ALU.add)
            else:
                nc.scalar.activation(dst, picked, ACT.Copy, scale=-0.5)

        def gather_other(t, c):
            gather_scaled((t, c) in ((3, 0),), other[c][:, t, :], a_rows[t], n1_sb, c)

        z_bf = [sb.tile([P, HALF * PACK], BF16, name="z_bf%d" % c, align_bytes=64) for c in range(2)]
        z_codes = [sb.tile([P, HALF], U32, name="z_codes%d" % c, align_bytes=64) for c in range(2)]
        z_scales = [sb.tile([P, HALF], U8, name="z_scales%d" % c, align_bytes=64) for c in range(2)]

        def combine(c, j, width):
            nc.vector.tensor_tensor(
                z_bf[c][:, PACK * j : PACK * (j + width)].rearrange("p (g i t) -> p g t i", t=PACK, i=2),
                gated[c][:, :, j : j + width].rearrange("p t (g i) -> p g t i", i=2),
                other[c][:, :, j : j + width].rearrange("p t (g i) -> p g t i", i=2),
                ALU.add,
            )

        def quantize(c, j, width):
            nc.vector.quantize_mx(
                out=z_codes[c][:, j : j + width].bitcast(FP8X4),
                scales=z_scales[c][:, j : j + width],
                in_=z_bf[c][:, PACK * j : PACK * (j + width)],
            )

        w_codes = sb.tile([P, N], U32, name="w_codes", align_bytes=64)
        w_scales = sb.tile([P, N], U8, name="w_scales", align_bytes=64)
        neg_h = [sb.tile([P, S], F32, name="neg_h%d" % t) for t in range(PACK)]
        h_left = [sb.tile([P, HALF], F32, name="h_left%d" % t) for t in range(PACK)]
        h_bank = {}

        def product_left(t):
            bank = mx_product(w_codes, w_scales, t, z_codes[0][:], z_scales[0][:])
            nc.scalar.activation(neg_h[t][:, cols_of(0)], bank[:], ACT.Copy, scale=-1.0)
            nc.scalar.copy(h_left[t][:], bank[:])

        def product_right(t, j, width):
            h_bank[t, j] = mx_product(w_codes, w_scales, t, z_codes[1][:, j : j + width], z_scales[1][:, j : j + width])

        def negate_right(engine, t, j, width):
            dst = neg_h[t][:, HALF + j : HALF + j + width]
            if engine == "V":
                nc.vector.tensor_scalar(dst, h_bank[t, j][:], -1.0, None, ALU.mult)
            else:
                nc.scalar.activation(dst, h_bank[t, j][:], ACT.Copy, scale=-1.0)

        for t in range(PACK):
            gated_product(t, 0, 0, HALF)
        gated_product(1, 1, 0, HALF)
        gated_product(2, 1, 0, HALF)
        for c in range(2):
            for t in range(PACK):
                gather_other(t, c)
        gated_product(3, 1, 0, HALF)
        nc.vector.quantize_mx(out=w_codes[:].bitcast(FP8X4), scales=w_scales[:], in_=w_bf[:])
        for j in (0, HALF // 2):
            combine(0, j, HALF // 2)
        for j in (0, HALF // 2):
            quantize(0, j, HALF // 2)
        for t in range(PACK):
            product_left(t)
        for j in (0, HALF // 2):
            gated_product(0, 1, j, HALF // 2)
        for j in (0, HALF // 2):
            combine(1, j, HALF // 2)
        for j in (0, HALF // 2):
            quantize(1, j, HALF // 2)

        out_rows = out.rearrange("(p t) n -> p t n", t=PACK)
        hop1 = {}
        st = [sb.tile([P, S], F32, name="st%d" % t, tag="st%d" % t) for t in range(PACK)]
        hop2 = [sb.tile([P, S], F32, name="hop2_%d" % t) for t in (0, 2, 3)]
        hop2_1 = [sb.tile([P, HALF], F32, name="hop2_1_%d" % c, tag="hop2_1_%d" % c) for c in range(2)]
        hop2_at = {(t, c): tile[:, cols_of(c)] for t, tile in zip((0, 2, 3), hop2) for c in range(2)}
        hop2_at[1, 0], hop2_at[1, 1] = hop2_1[0][:], hop2_1[1][:]

        def fused_hop(t):
            nc.vector.tensor_tensor(st[t][:, cols_of(0)], neg_h[t][:].indirect(half_of(n3_sb, 0)), h_left[t][:], ALU.add)

        def first_hop(engine, t, c):
            hop1[t, c] = ring.tile([P, HALF], F32, name="hop1")
            picked = neg_h[t][:].indirect(half_of(n3_sb, c))
            if engine == "S":
                nc.scalar.activation(hop1[t, c][:], picked, ACT.Copy)
            else:
                nc.vector.tensor_copy(hop1[t, c][:], picked)

        def add_hop(t, j, width):
            nc.vector.tensor_tensor(
                st[t][:, HALF + j : HALF + j + width], h_bank[t, j][:], hop1[t, 1][:, j : j + width], ALU.add
            )

        def second_hop(engine, t, c):
            gather_scaled(engine == "V", hop2_at[t, c], st[t], n3_sb, c)

        def finish(engine, t, cols, hop, res):
            engine.tensor_tensor(res, st[t][:, cols], hop, ALU.add)
            nc.sync.dma_start(out_rows[:, t, cols], res)

        for j in (0, HALF // 2):
            product_right(0, j, HALF // 2)
            negate_right("V", 0, j, HALF // 2)
        for t in range(1, PACK):
            product_right(t, 0, HALF)
        negate_right("S", 1, 0, HALF)
        fused_hop(0)
        first_hop("S", 0, 1)
        negate_right("S", 2, 0, HALF)
        fused_hop(1)
        add_hop(0, 0, HALF // 2)
        add_hop(0, HALF // 2, HALF // 2)
        first_hop("S", 1, 1)
        negate_right("S", 3, 0, HALF)
        fused_hop(2)
        add_hop(1, 0, HALF)
        fused_hop(3)
        for t in range(2):
            second_hop("S", t, 0)
            second_hop("S", t, 1)
        early = sb.tile([P, 3 * HALF], F32, name="early")
        finish(nc.gpsimd, 0, slice(0, S), hop2[0][:], early[:, 0:S])
        finish(nc.gpsimd, 1, cols_of(0), hop2_at[1, 0], early[:, S:])
        first_hop("V", 2, 1)
        first_hop("V", 3, 1)
        add_hop(2, 0, HALF)
        add_hop(3, 0, HALF)
        second_hop("S", 2, 0)
        second_hop("S", 2, 1)
        second_hop("V", 3, 1)
        second_hop("S", 3, 0)
        late = sb.tile([P, 5, HALF], F32, name="late", tag="hop2_1_0")
        for k, (t, c) in enumerate(((1, 1), (2, 0), (2, 1), (3, 1), (3, 0))):
            finish(nc.vector, t, cols_of(c), hop2_at[t, c], late[:, k, :])
